import numpy as np
CORES = [125,127,253,255,381,383,509,511]
N = 8
T, W, CAP = 8192, 64, 128
def entries(a): return a.T.reshape(-1)
def pack(v, P): return np.ascontiguousarray(np.asarray(v, np.int32).reshape(-1, P).T)
def lists(rng, how):
    L = rng.integers(0, T, (N, N, CAP))
    if how == "alike": L[:] = rng.integers(0, T, (N, N, 1))
    if how == "distinct": L = np.stack([np.stack([rng.permutation(T)[:CAP] for d in range(N)]) for r in range(N)])
    if how == "sorted": L = np.sort(L, axis=2)
    if how == "edge": L = np.where(rng.random((N, N, CAP)) < 0.5, 0, T - 1)
    return {"l": np.stack([pack(L[r].reshape(-1), 128) for r in range(N)])}
def setup_inputs(rng):
    return dict({"x": rng.standard_normal((N, T, W), dtype=np.float32)}, **lists(rng, "uniform"))
def setup_inputs_alike(rng):
    d = setup_inputs(rng); d.update(lists(rng, "alike"))
    for k in ("x",): d[k] = (d[k].astype(np.float32) * 1048576.0).astype(d[k].dtype)
    return d
def setup_inputs_distinct(rng):
    d = setup_inputs(rng); d.update(lists(rng, "distinct"))
    for k in ("x",): d[k] = (d[k].astype(np.float32) * (1 / 1024.0)).astype(d[k].dtype)
    return d
def setup_inputs_edge(rng):
    d = setup_inputs(rng); d.update(lists(rng, "edge"))
    return d
def setup_inputs_sorted(rng):
    d = setup_inputs(rng); d.update(lists(rng, "sorted"))
    return d
def check_inputs(x):
    bad = []
    if x["l"].min() < 0 or x["l"].max() >= T: bad.append("l out of range")
    return bad
def reference(x, l):
    y = np.zeros((N, N * CAP, W), x.dtype)
    for r in range(N):
        L = entries(l[r])
        for d in range(N): y[d][CAP * r:CAP * r + CAP] = x[r][L[CAP * d:CAP * d + CAP]]
    return {"y": y}

@@ -1,0 +1,158 @@
+from concourse.bass import DstId, RemoteDMATransfer, IndirectOffsetOnAxis
+
+N, ROWS, W, CAP = 8, 8192, 64, 128
+
+SCRATCH = {
+    "idx": ("sbuf", [128, N], "int32"),
+    "gat": ("sbuf", [128, N * W], "float32"),
+    "land": ("dram", [N, CAP, W], "float32"),
+    "rel": ("dram", [2, CAP, W], "float32"),
+}
+SEMAPHORES = (["lq", "lg", "sent", "stored", "arr_far", "arr_cable", "arr_switch", "arr_chip", "arr_rel"]
+              + ["gs%d" % d for d in range(N)])
+
+
+def _engines(topo, src, dst):
+    m = topo.mask(src, dst)
+    return [e for e in range(16) if (m >> e) & 1]
+
+
+def _bits(es):
+    m = 0
+    for e in es:
+        m |= 1 << e
+    return m
+
+
+def _same_chip(topo, a, b):
+    return topo.host(a) == topo.host(b) and topo.chip(a) == topo.chip(b)
+
+
+def _far(topo, T, s):
+    return [d for d in T.cores if d != s and not topo.may_write(s, d)]
+
+
+def _relay_of(topo, T, s):
+    far = _far(topo, T, s)
+    cand = [q for q in range(max(T.cores) + 1)
+            if T.rank_of(q) is None and topo.same_plane(s, q) and topo.chip(q) == topo.chip(s)
+            and topo.die(q) == topo.die(s) and topo.may_write(s, q)
+            and all(topo.may_write(q, d) and topo.chip(q) == topo.chip(d) for d in far)]
+    mine = [c for c in T.cores if _same_chip(topo, c, s)]
+    return cand[mine.index(s)]
+
+
+def _fused(g, T, topo, core, parts):
+    trs, n = [], 0
+    for src, dst, to, sem, es in parts:
+        rid, pid = topo.addr(to, core)
+        trs.append(RemoteDMATransfer(dst_ids=[DstId(rid=rid, pnc=pid)], dma_engine_mask=_bits(es), remote_sem=sem,
+                                     src=src, dst=dst))
+        n += len(es)
+    g.remote_dma_fused(trs, local_sem=T.sem.sent)
+    return n
+
+
+def _relay_program(g, core, T, topo, s):
+    far = _far(topo, T, s)
+    r = T.rank_of(s)
+    n_in = len(_engines(topo, s, core))
+    g.wait_ge(T.sem.arr_rel, n_in)
+    parts = []
+    for i, d in enumerate(far):
+        es = _engines(topo, core, d)
+        step = len(es) // 2
+        parts.append((T.rel[i], T.land[r], d, T.sem.arr_far, es[2 * i::step]))
+    n = _fused(g, T, topo, core, parts)
+    g.wait_ge(T.sem.sent, n)
+
+
+def rank_program(g, core, T, topo):
+    rank = T.rank_of(core)
+    if rank is None:
+        for s in T.cores:
+            if _relay_of(topo, T, s) == core:
+                _relay_program(g, core, T, topo, s)
+        return
+
+    others = [d for d in T.cores if d != core]
+    far = _far(topo, T, core)
+    chip = [d for d in others if _same_chip(topo, d, core)]
+    switch = [d for d in others if d not in chip and topo.same_plane(core, d)]
+    cable = [d for d in others if d not in far and d not in chip and d not in switch]
+    relay = _relay_of(topo, T, core)
+    R = T.rank_of
+
+    def blk(d):
+        return T.gat[:, W * R(d):W * R(d) + W]
+
+    def gather(d):
+        k = R(d)
+        g.indirect_dma_start(out=blk(d), out_offset=None, in_=T.x[:],
+                             in_offset=IndirectOffsetOnAxis(ap=T.idx[:, k:k + 1], axis=0),
+                             bounds_check=ROWS - 1, oob_is_err=True).then_inc(T.sem["gs%d" % k], 16)
+
+    def landed(ds):
+        for d in ds:
+            g.wait_ge(T.sem["gs%d" % R(d)], 16)
+
+    late = sorted(R(d) for d in chip + [core])
+    lo, hi = late[0], late[-1] + 1
+    g.dma_start(out=T.idx[:, lo:hi], in_=T.l[:, lo:hi]).then_inc(T.sem.lg, 16)
+    pieces = 0
+    if lo > 0:
+        g.sync.dma_start(out=T.idx[:, 0:lo], in_=T.l[:, 0:lo]).then_inc(T.sem.lq, 16)
+        pieces += 1
+    if hi < N:
+        g.scalar.dma_start(out=T.idx[:, hi:N], in_=T.l[:, hi:N]).then_inc(T.sem.lq, 16)
+        pieces += 1
+    g.wait_ge(T.sem.lq, 16 * pieces)
+
+    def pair(ds, sem, to=None, slots=None):
+        parts = []
+        for i, d in enumerate(ds):
+            tgt = d if to is None else to
+            es = _engines(topo, core, tgt)
+            dst = T.land[rank] if slots is None else slots[i]
+            parts.append((blk(d), dst, tgt, sem, es[i::len(ds)]))
+        return _fused(g, T, topo, core, parts)
+
+    sent = 0
+    gather(far[0]); gather(far[1]); gather(cable[0])
+    landed(far)
+    sent += pair(far, T.sem.arr_rel, to=relay, slots=[T.rel[0], T.rel[1]])
+    gather(cable[1]); gather(switch[0])
+    landed(cable)
+    sent += pair(cable, T.sem.arr_cable)
+    gather(switch[1])
+    g.wait_ge(T.sem.lg, 16)
+    gather(chip[0])
+    landed(switch)
+    sent += pair(switch, T.sem.arr_switch)
+    landed(chip)
+    out_es = _engines(topo, core, relay)
+    es = [e for e in _engines(topo, core, chip[0]) if e in out_es]
+    sent += _fused(g, T, topo, core, [(blk(chip[0]), T.land[rank], chip[0], T.sem.arr_chip, es)])
+    gather(core)
+
+    stores = [0]
+
+    def store(q, srcs, sem, count):
+        ks = sorted(R(s) for s in srcs)
+        q.wait_ge(sem, count)
+        q.dma_start(out=T.y[CAP * ks[0]:CAP * (ks[-1] + 1), :], in_=T.land[ks[0]:ks[-1] + 1]).then_inc(T.sem.stored, 16)
+        stores[0] += 1
+
+    def half(s):
+        return len(_engines(topo, s, core)) // 2
+
+    store(g.sync, cable, T.sem.arr_cable, sum(half(s) for s in cable))
+    store(g.sync, far, T.sem.arr_far, 2 * len(far))
+    store(g.sync, switch, T.sem.arr_switch, sum(half(s) for s in switch))
+    store(g.scalar, chip, T.sem.arr_chip, len(es))
+    g.scalar.wait_ge(T.sem["gs%d" % rank], 16)
+    g.scalar.dma_start(out=T.y[CAP * rank:CAP * (rank + 1), :], in_=blk(core)).then_inc(T.sem.stored, 16)
+    stores[0] += 1
+
+    g.wait_ge(T.sem.sent, sent)
+    g.wait_ge(T.sem.stored, 16 * stores[0])

@@ -2,14 +2,19 @@ from concourse.bass import DstId, RemoteDMATransfer, IndirectOffsetOnAxis
 
 N, ROWS, W, CAP = 8, 8192, 64, 128
 
+SCHED = [("g", "a"), ("g", "b"), ("g", "c"), ("s", "ab", (4, 4)), ("g", "d"), ("g", "e"),
+         ("s", "cd", (4, 4)), ("g", "f"), ("g", "n"), ("s", "ef", (4, 4)), ("g", "o"), ("s", "n", (8,))]
+RELAY_ENG = 2
+LATE = "no"
+
 SCRATCH = {
     "idx": ("sbuf", [128, N], "int32"),
     "gat": ("sbuf", [128, N * W], "float32"),
     "land": ("dram", [N, CAP, W], "float32"),
     "rel": ("dram", [2, CAP, W], "float32"),
 }
-SEMAPHORES = (["lq", "lg", "sent", "stored", "arr_far", "arr_cable", "arr_switch", "arr_chip", "arr_rel"]
-              + ["gs%d" % d for d in range(N)])
+SEMAPHORES = (["lq", "lg", "sent", "stored", "rel_a", "rel_b"] + ["arr_%s" % k for k in "abcdefn"]
+              + ["gs_%s" % k for k in "abcdefno"])
 
 
 def _engines(topo, src, dst):
@@ -28,18 +33,38 @@ def _same_chip(topo, a, b):
     return topo.host(a) == topo.host(b) and topo.chip(a) == topo.chip(b)
 
 
-def _far(topo, T, s):
-    return [d for d in T.cores if d != s and not topo.may_write(s, d)]
+def _place(topo, T, c):
+    return [x for x in T.cores if _same_chip(topo, x, c)].index(c)
+
+
+def _names(topo, T, s):
+    others = [d for d in T.cores if d != s]
+    far = [d for d in others if not topo.may_write(s, d)]
+    chip = [d for d in others if _same_chip(topo, d, s)]
+    switch = [d for d in others if d not in chip and topo.same_plane(s, d)]
+    cable = [d for d in others if d not in far and d not in chip and d not in switch]
+    p = _place(topo, T, s)
+
+    def order(ds):
+        return sorted(ds, key=lambda d: _place(topo, T, d) != p)
+    far, cable, switch = order(far), order(cable), order(switch)
+    return {"a": far[0], "b": far[1], "c": cable[0], "d": cable[1], "e": switch[0], "f": switch[1], "n": chip[0], "o": s}
 
 
 def _relay_of(topo, T, s):
-    far = _far(topo, T, s)
+    far = [d for d in T.cores if d != s and not topo.may_write(s, d)]
     cand = [q for q in range(max(T.cores) + 1)
             if T.rank_of(q) is None and topo.same_plane(s, q) and topo.chip(q) == topo.chip(s)
-            and topo.die(q) == topo.die(s) and topo.may_write(s, q)
+            and topo.die(q) != topo.die(s) and topo.may_write(s, q)
             and all(topo.may_write(q, d) and topo.chip(q) == topo.chip(d) for d in far)]
-    mine = [c for c in T.cores if _same_chip(topo, c, s)]
-    return cand[mine.index(s)]
+    mine = len([c for c in T.cores if _same_chip(topo, c, s)])
+    return cand[_place(topo, T, s) * (len(cand) // mine)]
+
+
+def _count(name):
+    for op in SCHED:
+        if op[0] == "s" and name in op[1]:
+            return op[2][op[1].index(name)]
 
 
 def _fused(g, T, topo, core, parts):
@@ -54,16 +79,19 @@ def _fused(g, T, topo, core, parts):
 
 
 def _relay_program(g, core, T, topo, s):
-    far = _far(topo, T, s)
+    to = _names(topo, T, s)
     r = T.rank_of(s)
-    n_in = len(_engines(topo, s, core))
-    g.wait_ge(T.sem.arr_rel, n_in)
-    parts = []
-    for i, d in enumerate(far):
-        es = _engines(topo, core, d)
-        step = len(es) // 2
-        parts.append((T.rel[i], T.land[r], d, T.sem.arr_far, es[2 * i::step]))
-    n = _fused(g, T, topo, core, parts)
+    n = 0
+    for op in SCHED:
+        ks = [k for k in op[1] if k in "ab"] if op[0] == "s" else []
+        parts = []
+        for i, k in enumerate(ks):
+            g.wait_ge(T.sem["rel_" + k], _count(k))
+            es = _engines(topo, core, to[k])
+            step = len(es) // RELAY_ENG
+            parts.append((T.rel["ab".index(k)], T.land[r], to[k], T.sem["arr_" + k], es[(step // 2) * i::step]))
+        if parts:
+            n += _fused(g, T, topo, core, parts)
     g.wait_ge(T.sem.sent, n)
 
 
@@ -75,28 +103,15 @@ def rank_program(g, core, T, topo):
                 _relay_program(g, core, T, topo, s)
         return
 
-    others = [d for d in T.cores if d != core]
-    far = _far(topo, T, core)
-    chip = [d for d in others if _same_chip(topo, d, core)]
-    switch = [d for d in others if d not in chip and topo.same_plane(core, d)]
-    cable = [d for d in others if d not in far and d not in chip and d not in switch]
+    to = _names(topo, T, core)
     relay = _relay_of(topo, T, core)
     R = T.rank_of
 
-    def blk(d):
-        return T.gat[:, W * R(d):W * R(d) + W]
+    def blk(k):
+        j = R(to[k])
+        return T.gat[:, W * j:W * j + W]
 
-    def gather(d):
-        k = R(d)
-        g.indirect_dma_start(out=blk(d), out_offset=None, in_=T.x[:],
-                             in_offset=IndirectOffsetOnAxis(ap=T.idx[:, k:k + 1], axis=0),
-                             bounds_check=ROWS - 1, oob_is_err=True).then_inc(T.sem["gs%d" % k], 16)
-
-    def landed(ds):
-        for d in ds:
-            g.wait_ge(T.sem["gs%d" % R(d)], 16)
-
-    late = sorted(R(d) for d in chip + [core])
+    late = sorted(R(to[k]) for k in LATE)
     lo, hi = late[0], late[-1] + 1
     g.dma_start(out=T.idx[:, lo:hi], in_=T.l[:, lo:hi]).then_inc(T.sem.lg, 16)
     pieces = 0
@@ -108,50 +123,45 @@ def rank_program(g, core, T, topo):
         pieces += 1
     g.wait_ge(T.sem.lq, 16 * pieces)
 
-    def pair(ds, sem, to=None, slots=None):
-        parts = []
-        for i, d in enumerate(ds):
-            tgt = d if to is None else to
-            es = _engines(topo, core, tgt)
-            dst = T.land[rank] if slots is None else slots[i]
-            parts.append((blk(d), dst, tgt, sem, es[i::len(ds)]))
-        return _fused(g, T, topo, core, parts)
-
-    sent = 0
-    gather(far[0]); gather(far[1]); gather(cable[0])
-    landed(far)
-    sent += pair(far, T.sem.arr_rel, to=relay, slots=[T.rel[0], T.rel[1]])
-    gather(cable[1]); gather(switch[0])
-    landed(cable)
-    sent += pair(cable, T.sem.arr_cable)
-    gather(switch[1])
-    g.wait_ge(T.sem.lg, 16)
-    gather(chip[0])
-    landed(switch)
-    sent += pair(switch, T.sem.arr_switch)
-    landed(chip)
-    out_es = _engines(topo, core, relay)
-    es = [e for e in _engines(topo, core, chip[0]) if e in out_es]
-    sent += _fused(g, T, topo, core, [(blk(chip[0]), T.land[rank], chip[0], T.sem.arr_chip, es)])
-    gather(core)
+    pool = _engines(topo, core, relay)
+    sent, lg_waited = 0, False
+    for op in SCHED:
+        if op[0] == "g":
+            k = op[1]
+            if k in LATE and not lg_waited:
+                g.wait_ge(T.sem.lg, 16)
+                lg_waited = True
+            j = R(to[k])
+            g.indirect_dma_start(out=blk(k), out_offset=None, in_=T.x[:],
+                                 in_offset=IndirectOffsetOnAxis(ap=T.idx[:, j:j + 1], axis=0),
+                                 bounds_check=ROWS - 1, oob_is_err=True).then_inc(T.sem["gs_" + k], 16)
+        else:
+            parts, at = [], 0
+            for k, ne in zip(op[1], op[2]):
+                g.wait_ge(T.sem["gs_" + k], 16)
+                es = pool[at:at + ne]
+                at += ne
+                if k in "ab":
+                    parts.append((blk(k), T.rel["ab".index(k)], relay, T.sem["rel_" + k], es))
+                else:
+                    parts.append((blk(k), T.land[rank], to[k], T.sem["arr_" + k], es))
+            sent += _fused(g, T, topo, core, parts)
 
     stores = [0]
 
-    def store(q, srcs, sem, count):
-        ks = sorted(R(s) for s in srcs)
-        q.wait_ge(sem, count)
-        q.dma_start(out=T.y[CAP * ks[0]:CAP * (ks[-1] + 1), :], in_=T.land[ks[0]:ks[-1] + 1]).then_inc(T.sem.stored, 16)
+    def store(q, ks):
+        js = sorted(R(to[k]) for k in ks)
+        for k in ks:
+            q.wait_ge(T.sem["arr_" + k], RELAY_ENG if k in "ab" else _count(k))
+        q.dma_start(out=T.y[CAP * js[0]:CAP * (js[-1] + 1), :], in_=T.land[js[0]:js[-1] + 1]).then_inc(T.sem.stored, 16)
         stores[0] += 1
 
-    def half(s):
-        return len(_engines(topo, s, core)) // 2
-
-    store(g.sync, cable, T.sem.arr_cable, sum(half(s) for s in cable))
-    store(g.sync, far, T.sem.arr_far, 2 * len(far))
-    store(g.sync, switch, T.sem.arr_switch, sum(half(s) for s in switch))
-    store(g.scalar, chip, T.sem.arr_chip, len(es))
-    g.scalar.wait_ge(T.sem["gs%d" % rank], 16)
-    g.scalar.dma_start(out=T.y[CAP * rank:CAP * (rank + 1), :], in_=blk(core)).then_inc(T.sem.stored, 16)
+    store(g.sync, "cd")
+    store(g.sync, "ef")
+    store(g.sync, "n")
+    store(g.scalar, "ab")
+    g.scalar.wait_ge(T.sem.gs_o, 16)
+    g.scalar.dma_start(out=T.y[CAP * rank:CAP * (rank + 1), :], in_=blk("o")).then_inc(T.sem.stored, 16)
     stores[0] += 1
 
     g.wait_ge(T.sem.sent, sent)

@@ -1,20 +1,45 @@
 from concourse.bass import DstId, RemoteDMATransfer, IndirectOffsetOnAxis
+from concourse.mybir import AluOpType, ActivationFunctionType
 
 N, ROWS, W, CAP = 8, 8192, 64, 128
 
-SCHED = [("g", "a"), ("g", "b"), ("g", "c"), ("s", "ab", (4, 4)), ("g", "d"), ("g", "e"),
-         ("s", "cd", (4, 4)), ("g", "f"), ("g", "n"), ("s", "ef", (4, 4)), ("g", "o"), ("s", "n", (8,))]
+SCHED = [("g", "a"), ("g", "b"), ("g", "c"), ("s", "ab", (4, 4)), ("g", "d"),
+         ("s", "cd", (4, 4)), ("s", "ef", (4, 4)), ("s", "n", (8,))]
+VPAIRS = ["ef", "no"]
+VLISTS = "".join(VPAIRS)
 RELAY_ENG = 2
-LATE = "no"
+
+NCH = 8
+FREE = ROWS * W // 128
+CW = FREE // NCH
+RPC = ROWS // NCH
+KB = (RPC // 128).bit_length() - 1
+ND = len(VLISTS)
 
 SCRATCH = {
     "idx": ("sbuf", [128, N], "int32"),
+    "idv": ("sbuf", [128, N], "int32"),
     "gat": ("sbuf", [128, N * W], "float32"),
     "land": ("dram", [N, CAP, W], "float32"),
     "rel": ("dram", [2, CAP, W], "float32"),
+    "xs": ("sbuf", [128, FREE], "float32"),
+    "xt": ("sbuf", [128, FREE + 4], "float32"),
+    "w1": ("sbuf", [128, 128], "int32"), "w1a": ("sbuf", [128, 128], "int32"), "w1b": ("sbuf", [128, 32], "int32"),
+    "w2": ("sbuf", [128, 8], "int32"), "w2a": ("sbuf", [128, 8], "int32"), "pq": ("sbuf", [128, 1], "int32"),
+    "rep": ("sbuf", [128, 128], "float32"), "sel": ("sbuf", [128, 32], "float32"), "dm8": ("sbuf", [128, 8], "float32"),
+    "ap32": ("sbuf", [128, 1], "float32"),
+    "rf": ("sbuf", [128, N], "float32"), "vm": ("sbuf", [128, 8 * ND], "float32"),
+    "rr": ("sbuf", [128, 8 * ND], "int32"), "ta": ("sbuf", [128, 8 * ND], "int32"), "tb": ("sbuf", [128, 8 * ND], "int32"),
+    "tc": ("sbuf", [128, 8 * ND], "int32"), "tq": ("sbuf", [128, 8 * ND], "int32"),
+    "off": ("sbuf", [128, 16 * ND], "uint16"),
+    "gv": ("sbuf", [128, 256 * ND], "float32"),
+    "pso": ("psum", [128, 512], "float32"),
+    "ps_e": ("psum", [128, 512], "float32"), "ps_f": ("psum", [128, 512], "float32"),
+    "ps_n": ("psum", [128, 512], "float32"), "ps_o": ("psum", [128, 512], "float32"),
 }
-SEMAPHORES = (["lq", "lg", "sent", "stored", "rel_a", "rel_b"] + ["arr_%s" % k for k in "abcdefn"]
-              + ["gs_%s" % k for k in "abcdefno"])
+SEMAPHORES = (["lq", "lg", "sent", "stored", "rel_a", "rel_b", "gi", "vs", "vmd", "ts", "gv_0", "gv_1"]
+              + ["arr_%s" % k for k in "abcdefn"] + ["gs_%s" % k for k in "abcdefno"]
+              + ["pe_%s" % k for k in "efno"] + ["ev_%s" % k for k in "efno"] + ["xq_%d" % q for q in range(NCH)])
 
 
 def _engines(topo, src, dst):
@@ -95,6 +120,72 @@ def _relay_program(g, core, T, topo, s):
     g.wait_ge(T.sem.sent, n)
 
 
+def _vector_path(g, T, cols):
+    V, P = g.vector, g.tensor
+    A = AluOpType
+    nv = [0]
+
+    def vi(ins):
+        ins.then_inc(T.sem.vs, 1)
+        nv[0] += 1
+
+    def vsync():
+        V.wait_ge(T.sem.vs, nv[0])
+
+    V.wait_ge(T.sem.gi, 2)
+    vi(V.tensor_scalar(T.w1a[:, :], T.w1[:, :], 15, None, A.bitwise_and))
+    vi(V.tensor_scalar(T.w1b[:, :], T.w1[:, 0:32], 31, None, A.bitwise_and))
+    vi(V.tensor_scalar(T.w2a[:, :], T.w2[:, :], 4, None, A.arith_shift_right))
+    vi(V.tensor_scalar(T.pq[:, :], T.w2[:, 0:1], 96, None, A.bitwise_and))
+    vi(V.memset(T.xt[:, FREE:FREE + 4], 0.0))
+    vsync()
+    vi(V.tensor_scalar(T.rep[:, :], T.w1a[:, :], 0, None, A.is_equal))
+    vi(V.tensor_scalar(T.sel[:, :], T.w1b[:, :], 0, None, A.is_equal))
+    vi(V.tensor_scalar(T.dm8[:, :], T.w2a[:, :], 0, None, A.is_equal))
+    vi(V.tensor_copy(T.ap32[:, :], T.pq[:, :]))
+    lo, hi = min(cols), max(cols) + 1
+    V.wait_ge(T.sem.lg, 16)
+    vi(V.tensor_copy(T.rf[:, lo:hi], T.idv[:, lo:hi]))
+    vsync()
+    for i, j in enumerate(cols):
+        V.tensor_scalar(T.vm[:, 8 * i:8 * i + 8], T.dm8[:, :], T.rf[:, j:j + 1], None, A.mult).then_inc(T.sem.vmd, 1)
+    P.wait_ge(T.sem.vmd, ND)
+    P.matmul(T.pso[:, 0:8 * ND], T.rep[:, :], T.vm[:, :], True, True).then_inc(T.sem.ts, 1)
+    V.wait_ge(T.sem.ts, 1)
+    vi(V.tensor_copy(T.rr[:, :], T.pso[:, 0:8 * ND]))
+    vsync()
+    vi(V.tensor_scalar(T.ta[:, :], T.rr[:, :], (ROWS - 1) - (RPC - 1), 1, A.bitwise_and, A.logical_shift_right))
+    vi(V.tensor_scalar(T.tb[:, :], T.rr[:, :], (1 << KB) - 1, None, A.bitwise_and))
+    vi(V.tensor_scalar(T.tc[:, :], T.rr[:, :], KB, 31, A.logical_shift_right, A.bitwise_and))
+    vi(V.tensor_scalar(T.tq[:, :], T.rr[:, :], KB, 96, A.logical_shift_right, A.bitwise_and))
+    vsync()
+    vi(V.tensor_scalar(T.tq[:, :], T.tq[:, :], T.ap32[:, 0:1], 2 * FREE, A.not_equal, A.mult))
+    vi(V.tensor_scalar(T.tb[:, :], T.tb[:, :], W, None, A.mult))
+    vi(V.tensor_tensor(T.ta[:, :], T.ta[:, :], T.tc[:, :], A.add))
+    vsync()
+    vi(V.tensor_tensor(T.tb[:, :], T.tb[:, :], T.tq[:, :], A.add))
+    vsync()
+    vi(V.tensor_tensor(T.ta[:, :], T.ta[:, :], T.tb[:, :], A.add))
+    vsync()
+    for s in range(len(VPAIRS)):
+        for h in range(2):
+            vi(V.tensor_scalar(T.off[:, 32 * s + 16 * h:32 * s + 16 * h + 16], T.ta[:, 16 * s:16 * s + 16],
+                               32 * h, FREE, A.add, A.min))
+    for q in range(NCH):
+        V.wait_ge(T.sem["xq_%d" % q], 16)
+        vi(V.transpose(T.xt[:, CW * q:CW * q + CW], T.xs[:, CW * q:CW * q + CW]))
+    vsync()
+    for s, pair in enumerate(VPAIRS):
+        V.tensor_copy(T.gv[:, 512 * s:512 * s + 512],
+                      T.xt[:, 0:FREE + 4].indirect(T.off[:, 32 * s:32 * s + 32])).then_inc(T.sem["gv_%d" % s], 1)
+        P.wait_ge(T.sem["gv_%d" % s], 1)
+        for i, k in enumerate(pair):
+            for h in range(2):
+                at = 512 * s + 256 * h + 128 * i
+                P.matmul(T["ps_" + k][:, 32 * h:32 * h + 32], T.gv[:, at:at + 128], T.sel[:, :],
+                         True, True).then_inc(T.sem["pe_" + k], 1)
+
+
 def rank_program(g, core, T, topo):
     rank = T.rank_of(core)
     if rank is None:
@@ -111,26 +202,23 @@ def rank_program(g, core, T, topo):
         j = R(to[k])
         return T.gat[:, W * j:W * j + W]
 
-    late = sorted(R(to[k]) for k in LATE)
-    lo, hi = late[0], late[-1] + 1
-    g.dma_start(out=T.idx[:, lo:hi], in_=T.l[:, lo:hi]).then_inc(T.sem.lg, 16)
-    pieces = 0
-    if lo > 0:
-        g.sync.dma_start(out=T.idx[:, 0:lo], in_=T.l[:, 0:lo]).then_inc(T.sem.lq, 16)
-        pieces += 1
-    if hi < N:
-        g.scalar.dma_start(out=T.idx[:, hi:N], in_=T.l[:, hi:N]).then_inc(T.sem.lq, 16)
-        pieces += 1
-    g.wait_ge(T.sem.lq, 16 * pieces)
+    cols = [R(to[k]) for k in VLISTS]
+    lo, hi = min(cols), max(cols) + 1
+    g.sync.dma_start(out=T.idx[:, :], in_=T.l[:, :]).then_inc(T.sem.lq, 16)
+    g.dma_start(out=T.idv[:, lo:hi], in_=T.l[:, lo:hi]).then_inc(T.sem.lg, 16)
+    for q in range(NCH):
+        (g.scalar if q % 2 == 0 else g.sync).dma_start(out=T.xs[:, CW * q:CW * q + CW],
+                                                       in_=T.x[RPC * q:RPC * q + RPC, :]).then_inc(T.sem["xq_%d" % q], 16)
+    g.iota(T.w1[:, :], [[1, 128]], 128, -1).then_inc(T.sem.gi, 1)
+    g.iota(T.w2[:, :], [[-16, 8]], 0, 1).then_inc(T.sem.gi, 1)
+    _vector_path(g, T, cols)
+    g.wait_ge(T.sem.lq, 16)
 
     pool = _engines(topo, core, relay)
-    sent, lg_waited = 0, False
+    sent = 0
     for op in SCHED:
         if op[0] == "g":
             k = op[1]
-            if k in LATE and not lg_waited:
-                g.wait_ge(T.sem.lg, 16)
-                lg_waited = True
             j = R(to[k])
             g.indirect_dma_start(out=blk(k), out_offset=None, in_=T.x[:],
                                  in_offset=IndirectOffsetOnAxis(ap=T.idx[:, j:j + 1], axis=0),
@@ -138,7 +226,10 @@ def rank_program(g, core, T, topo):
         else:
             parts, at = [], 0
             for k, ne in zip(op[1], op[2]):
-                g.wait_ge(T.sem["gs_" + k], 16)
+                if k in VLISTS:
+                    g.wait_ge(T.sem["ev_" + k], 1)
+                else:
+                    g.wait_ge(T.sem["gs_" + k], 16)
                 es = pool[at:at + ne]
                 at += ne
                 if k in "ab":
@@ -146,6 +237,10 @@ def rank_program(g, core, T, topo):
                 else:
                     parts.append((blk(k), T.land[rank], to[k], T.sem["arr_" + k], es))
             sent += _fused(g, T, topo, core, parts)
+
+    for k in VLISTS:
+        g.scalar.wait_ge(T.sem["pe_" + k], 2)
+        g.scalar.activation(blk(k), T["ps_" + k][:, 0:W], ActivationFunctionType.Copy).then_inc(T.sem["ev_" + k], 1)
 
     stores = [0]
 
@@ -156,13 +251,13 @@ def rank_program(g, core, T, topo):
         q.dma_start(out=T.y[CAP * js[0]:CAP * (js[-1] + 1), :], in_=T.land[js[0]:js[-1] + 1]).then_inc(T.sem.stored, 16)
         stores[0] += 1
 
-    store(g.sync, "cd")
-    store(g.sync, "ef")
-    store(g.sync, "n")
-    store(g.scalar, "ab")
-    g.scalar.wait_ge(T.sem.gs_o, 16)
+    g.scalar.wait_ge(T.sem.ev_o, 1)
     g.scalar.dma_start(out=T.y[CAP * rank:CAP * (rank + 1), :], in_=blk("o")).then_inc(T.sem.stored, 16)
     stores[0] += 1
+    store(g.sync, "ab")
+    store(g.sync, "cd")
+    store(g.sync, "ef")
+    store(g.scalar, "n")
 
     g.wait_ge(T.sem.sent, sent)
     g.wait_ge(T.sem.stored, 16 * stores[0])

@@ -3,11 +3,12 @@ from concourse.mybir import AluOpType, ActivationFunctionType
 
 N, ROWS, W, CAP = 8, 8192, 64, 128
 
-SCHED = [("g", "a"), ("g", "b"), ("g", "c"), ("s", "ab", (4, 4)), ("g", "d"),
+SCHED = [("g", "a"), ("g", "b"), ("s", "a", (8,)), ("s", "b", (8,)),
          ("s", "cd", (4, 4)), ("s", "ef", (4, 4)), ("s", "n", (8,))]
-VPAIRS = ["ef", "no"]
+VPAIRS = ["cd", "ef", "no"]
 VLISTS = "".join(VPAIRS)
-RELAY_ENG = 2
+GLISTS = "".join(op[1] for op in SCHED if op[0] == "g")
+RELAY_ENG = 4
 
 NCH = 8
 FREE = ROWS * W // 128
@@ -15,15 +16,15 @@ CW = FREE // NCH
 RPC = ROWS // NCH
 KB = (RPC // 128).bit_length() - 1
 ND = len(VLISTS)
+EARLY = 2
 
 SCRATCH = {
     "idx": ("sbuf", [128, N], "int32"),
-    "idv": ("sbuf", [128, N], "int32"),
     "gat": ("sbuf", [128, N * W], "float32"),
     "land": ("dram", [N, CAP, W], "float32"),
     "rel": ("dram", [2, CAP, W], "float32"),
     "xs": ("sbuf", [128, FREE], "float32"),
-    "xt": ("sbuf", [128, FREE + 4], "float32"),
+    "xt": ("sbuf", [128, FREE + 36], "float32"),
     "w1": ("sbuf", [128, 128], "int32"), "w1a": ("sbuf", [128, 128], "int32"), "w1b": ("sbuf", [128, 32], "int32"),
     "w2": ("sbuf", [128, 8], "int32"), "w2a": ("sbuf", [128, 8], "int32"), "pq": ("sbuf", [128, 1], "int32"),
     "rep": ("sbuf", [128, 128], "float32"), "sel": ("sbuf", [128, 32], "float32"), "dm8": ("sbuf", [128, 8], "float32"),
@@ -31,15 +32,16 @@ SCRATCH = {
     "rf": ("sbuf", [128, N], "float32"), "vm": ("sbuf", [128, 8 * ND], "float32"),
     "rr": ("sbuf", [128, 8 * ND], "int32"), "ta": ("sbuf", [128, 8 * ND], "int32"), "tb": ("sbuf", [128, 8 * ND], "int32"),
     "tc": ("sbuf", [128, 8 * ND], "int32"), "tq": ("sbuf", [128, 8 * ND], "int32"),
-    "off": ("sbuf", [128, 16 * ND], "uint16"),
+    "off": ("sbuf", [128, 8 * ND], "uint16"),
     "gv": ("sbuf", [128, 256 * ND], "float32"),
     "pso": ("psum", [128, 512], "float32"),
-    "ps_e": ("psum", [128, 512], "float32"), "ps_f": ("psum", [128, 512], "float32"),
-    "ps_n": ("psum", [128, 512], "float32"), "ps_o": ("psum", [128, 512], "float32"),
 }
-SEMAPHORES = (["lq", "lg", "sent", "stored", "rel_a", "rel_b", "gi", "vs", "vmd", "ts", "gv_0", "gv_1"]
-              + ["arr_%s" % k for k in "abcdefn"] + ["gs_%s" % k for k in "abcdefno"]
-              + ["pe_%s" % k for k in "efno"] + ["ev_%s" % k for k in "efno"] + ["xq_%d" % q for q in range(NCH)])
+for _k in VLISTS:
+    SCRATCH["ps_" + _k] = ("psum", [128, 512], "float32")
+SEMAPHORES = (["lq", "sent", "stored", "rel_a", "rel_b", "gi", "vs", "vmd", "ts"]
+              + ["gv_%d" % s for s in range(len(VPAIRS))]
+              + ["arr_%s" % k for k in "abcdefn"] + ["gs_%s" % k for k in GLISTS]
+              + ["pe_%s" % k for k in VLISTS] + ["ev_%s" % k for k in VLISTS] + ["xq_%d" % q for q in range(NCH)])
 
 
 def _engines(topo, src, dst):
@@ -120,8 +122,8 @@ def _relay_program(g, core, T, topo, s):
     g.wait_ge(T.sem.sent, n)
 
 
-def _vector_path(g, T, cols):
-    V, P = g.vector, g.tensor
+def _vector_path(g, T, cols, blk):
+    V, P, S = g.vector, g.tensor, g.scalar
     A = AluOpType
     nv = [0]
 
@@ -132,25 +134,30 @@ def _vector_path(g, T, cols):
     def vsync():
         V.wait_ge(T.sem.vs, nv[0])
 
+    def turn(q):
+        V.wait_ge(T.sem["xq_%d" % q], 16)
+        vi(V.transpose(T.xt[:, CW * q:CW * q + CW], T.xs[:, CW * q:CW * q + CW]))
+
     V.wait_ge(T.sem.gi, 2)
     vi(V.tensor_scalar(T.w1a[:, :], T.w1[:, :], 15, None, A.bitwise_and))
     vi(V.tensor_scalar(T.w1b[:, :], T.w1[:, 0:32], 31, None, A.bitwise_and))
     vi(V.tensor_scalar(T.w2a[:, :], T.w2[:, :], 4, None, A.arith_shift_right))
     vi(V.tensor_scalar(T.pq[:, :], T.w2[:, 0:1], 96, None, A.bitwise_and))
-    vi(V.memset(T.xt[:, FREE:FREE + 4], 0.0))
+    vi(V.memset(T.xt[:, FREE:FREE + 36], 0.0))
     vsync()
     vi(V.tensor_scalar(T.rep[:, :], T.w1a[:, :], 0, None, A.is_equal))
     vi(V.tensor_scalar(T.sel[:, :], T.w1b[:, :], 0, None, A.is_equal))
     vi(V.tensor_scalar(T.dm8[:, :], T.w2a[:, :], 0, None, A.is_equal))
     vi(V.tensor_copy(T.ap32[:, :], T.pq[:, :]))
-    lo, hi = min(cols), max(cols) + 1
-    V.wait_ge(T.sem.lg, 16)
-    vi(V.tensor_copy(T.rf[:, lo:hi], T.idv[:, lo:hi]))
+    V.wait_ge(T.sem.lq, 16)
+    vi(V.tensor_copy(T.rf[:, :], T.idx[:, :]))
     vsync()
     for i, j in enumerate(cols):
         V.tensor_scalar(T.vm[:, 8 * i:8 * i + 8], T.dm8[:, :], T.rf[:, j:j + 1], None, A.mult).then_inc(T.sem.vmd, 1)
     P.wait_ge(T.sem.vmd, ND)
     P.matmul(T.pso[:, 0:8 * ND], T.rep[:, :], T.vm[:, :], True, True).then_inc(T.sem.ts, 1)
+    for q in range(EARLY):
+        turn(q)
     V.wait_ge(T.sem.ts, 1)
     vi(V.tensor_copy(T.rr[:, :], T.pso[:, 0:8 * ND]))
     vsync()
@@ -167,23 +174,40 @@ def _vector_path(g, T, cols):
     vsync()
     vi(V.tensor_tensor(T.ta[:, :], T.ta[:, :], T.tb[:, :], A.add))
     vsync()
-    for s in range(len(VPAIRS)):
-        for h in range(2):
-            vi(V.tensor_scalar(T.off[:, 32 * s + 16 * h:32 * s + 16 * h + 16], T.ta[:, 16 * s:16 * s + 16],
-                               32 * h, FREE, A.add, A.min))
-    for q in range(NCH):
-        V.wait_ge(T.sem["xq_%d" % q], 16)
-        vi(V.transpose(T.xt[:, CW * q:CW * q + CW], T.xs[:, CW * q:CW * q + CW]))
+    vi(V.tensor_scalar(T.off[:, :], T.ta[:, :], FREE, None, A.min))
+    for q in range(EARLY, NCH):
+        turn(q)
     vsync()
+    S.wait_ge(T.sem.vs, nv[0])
+
+    def gather(s, h):
+        out = T.gv[:, 512 * s + 256 * h:512 * s + 256 * h + 256]
+        src = T.xt[:, 32 * h:32 * h + FREE + 4].indirect(T.off[:, 16 * s:16 * s + 16])
+        ins = V.tensor_copy(out, src) if h == 0 else S.activation(out, src, ActivationFunctionType.Copy)
+        ins.then_inc(T.sem["gv_%d" % s], 1)
+
+    def leave(on_vector, k):
+        (V if on_vector else S).wait_ge(T.sem["pe_" + k], 2)
+        ins = (V.tensor_copy(blk(k), T["ps_" + k][:, 0:W]) if on_vector
+               else S.activation(blk(k), T["ps_" + k][:, 0:W], ActivationFunctionType.Copy))
+        ins.then_inc(T.sem["ev_" + k], 1)
+
     for s, pair in enumerate(VPAIRS):
-        V.tensor_copy(T.gv[:, 512 * s:512 * s + 512],
-                      T.xt[:, 0:FREE + 4].indirect(T.off[:, 32 * s:32 * s + 32])).then_inc(T.sem["gv_%d" % s], 1)
-        P.wait_ge(T.sem["gv_%d" % s], 1)
+        gather(s, 0)
+        P.wait_ge(T.sem["gv_%d" % s], 2)
         for i, k in enumerate(pair):
             for h in range(2):
                 at = 512 * s + 256 * h + 128 * i
                 P.matmul(T["ps_" + k][:, 32 * h:32 * h + 32], T.gv[:, at:at + 128], T.sel[:, :],
                          True, True).then_inc(T.sem["pe_" + k], 1)
+    last = len(VPAIRS) - 1
+    gather(0, 1)
+    for s in range(last):
+        gather(s + 1, 1)
+        for k in VPAIRS[s]:
+            leave(False, k)
+    for k in VPAIRS[last]:
+        leave(True, k)
 
 
 def rank_program(g, core, T, topo):
@@ -203,15 +227,13 @@ def rank_program(g, core, T, topo):
         return T.gat[:, W * j:W * j + W]
 
     cols = [R(to[k]) for k in VLISTS]
-    lo, hi = min(cols), max(cols) + 1
     g.sync.dma_start(out=T.idx[:, :], in_=T.l[:, :]).then_inc(T.sem.lq, 16)
-    g.dma_start(out=T.idv[:, lo:hi], in_=T.l[:, lo:hi]).then_inc(T.sem.lg, 16)
     for q in range(NCH):
         (g.scalar if q % 2 == 0 else g.sync).dma_start(out=T.xs[:, CW * q:CW * q + CW],
                                                        in_=T.x[RPC * q:RPC * q + RPC, :]).then_inc(T.sem["xq_%d" % q], 16)
     g.iota(T.w1[:, :], [[1, 128]], 128, -1).then_inc(T.sem.gi, 1)
     g.iota(T.w2[:, :], [[-16, 8]], 0, 1).then_inc(T.sem.gi, 1)
-    _vector_path(g, T, cols)
+    _vector_path(g, T, cols, blk)
     g.wait_ge(T.sem.lq, 16)
 
     pool = _engines(topo, core, relay)
@@ -238,10 +260,6 @@ def rank_program(g, core, T, topo):
                     parts.append((blk(k), T.land[rank], to[k], T.sem["arr_" + k], es))
             sent += _fused(g, T, topo, core, parts)
 
-    for k in VLISTS:
-        g.scalar.wait_ge(T.sem["pe_" + k], 2)
-        g.scalar.activation(blk(k), T["ps_" + k][:, 0:W], ActivationFunctionType.Copy).then_inc(T.sem["ev_" + k], 1)
-
     stores = [0]
 
     def store(q, ks):
@@ -255,7 +273,7 @@ def rank_program(g, core, T, topo):
     g.scalar.dma_start(out=T.y[CAP * rank:CAP * (rank + 1), :], in_=blk("o")).then_inc(T.sem.stored, 16)
     stores[0] += 1
     store(g.sync, "ab")
-    store(g.sync, "cd")
+    store(g.scalar, "cd")
     store(g.sync, "ef")
     store(g.scalar, "n")
 

from concourse.bass import DstId, RemoteDMATransfer, IndirectOffsetOnAxis
from concourse.mybir import AluOpType, ActivationFunctionType

N, ROWS, W, CAP = 8, 8192, 64, 128

SCHED = [("g", "a"), ("g", "b"), ("s", "a", (8,)), ("s", "b", (8,)),
         ("s", "cd", (4, 4)), ("s", "ef", (4, 4)), ("s", "n", (8,))]
VPAIRS = ["cd", "ef", "no"]
VLISTS = "".join(VPAIRS)
GLISTS = "".join(op[1] for op in SCHED if op[0] == "g")
RELAY_ENG = 4

NCH = 8
FREE = ROWS * W // 128
CW = FREE // NCH
RPC = ROWS // NCH
KB = (RPC // 128).bit_length() - 1
ND = len(VLISTS)
EARLY = 2

SCRATCH = {
    "idx": ("sbuf", [128, N], "int32"),
    "gat": ("sbuf", [128, N * W], "float32"),
    "land": ("dram", [N, CAP, W], "float32"),
    "rel": ("dram", [2, CAP, W], "float32"),
    "xs": ("sbuf", [128, FREE], "float32"),
    "xt": ("sbuf", [128, FREE + 36], "float32"),
    "w1": ("sbuf", [128, 128], "int32"), "w1a": ("sbuf", [128, 128], "int32"), "w1b": ("sbuf", [128, 32], "int32"),
    "w2": ("sbuf", [128, 8], "int32"), "w2a": ("sbuf", [128, 8], "int32"), "pq": ("sbuf", [128, 1], "int32"),
    "rep": ("sbuf", [128, 128], "float32"), "sel": ("sbuf", [128, 32], "float32"), "dm8": ("sbuf", [128, 8], "float32"),
    "ap32": ("sbuf", [128, 1], "float32"),
    "rf": ("sbuf", [128, N], "float32"), "vm": ("sbuf", [128, 8 * ND], "float32"),
    "rr": ("sbuf", [128, 8 * ND], "int32"), "ta": ("sbuf", [128, 8 * ND], "int32"), "tb": ("sbuf", [128, 8 * ND], "int32"),
    "tc": ("sbuf", [128, 8 * ND], "int32"), "tq": ("sbuf", [128, 8 * ND], "int32"),
    "off": ("sbuf", [128, 8 * ND], "uint16"),
    "gv": ("sbuf", [128, 256 * ND], "float32"),
    "pso": ("psum", [128, 512], "float32"),
}
for _k in VLISTS:
    SCRATCH["ps_" + _k] = ("psum", [128, 512], "float32")
SEMAPHORES = (["lq", "sent", "stored", "rel_a", "rel_b", "gi", "vs", "vmd", "ts"]
              + ["gv_%d" % s for s in range(len(VPAIRS))]
              + ["arr_%s" % k for k in "abcdefn"] + ["gs_%s" % k for k in GLISTS]
              + ["pe_%s" % k for k in VLISTS] + ["ev_%s" % k for k in VLISTS] + ["xq_%d" % q for q in range(NCH)])


def _engines(topo, src, dst):
    m = topo.mask(src, dst)
    return [e for e in range(16) if (m >> e) & 1]


def _bits(es):
    m = 0
    for e in es:
        m |= 1 << e
    return m


def _same_chip(topo, a, b):
    return topo.host(a) == topo.host(b) and topo.chip(a) == topo.chip(b)


def _place(topo, T, c):
    return [x for x in T.cores if _same_chip(topo, x, c)].index(c)


def _names(topo, T, s):
    others = [d for d in T.cores if d != s]
    far = [d for d in others if not topo.may_write(s, d)]
    chip = [d for d in others if _same_chip(topo, d, s)]
    switch = [d for d in others if d not in chip and topo.same_plane(s, d)]
    cable = [d for d in others if d not in far and d not in chip and d not in switch]
    p = _place(topo, T, s)

    def order(ds):
        return sorted(ds, key=lambda d: _place(topo, T, d) != p)
    far, cable, switch = order(far), order(cable), order(switch)
    return {"a": far[0], "b": far[1], "c": cable[0], "d": cable[1], "e": switch[0], "f": switch[1], "n": chip[0], "o": s}


def _relay_of(topo, T, s):
    far = [d for d in T.cores if d != s and not topo.may_write(s, d)]
    cand = [q for q in range(max(T.cores) + 1)
            if T.rank_of(q) is None and topo.same_plane(s, q) and topo.chip(q) == topo.chip(s)
            and topo.die(q) != topo.die(s) and topo.may_write(s, q)
            and all(topo.may_write(q, d) and topo.chip(q) == topo.chip(d) for d in far)]
    mine = len([c for c in T.cores if _same_chip(topo, c, s)])
    return cand[_place(topo, T, s) * (len(cand) // mine)]


def _count(name):
    for op in SCHED:
        if op[0] == "s" and name in op[1]:
            return op[2][op[1].index(name)]


def _fused(g, T, topo, core, parts):
    trs, n = [], 0
    for src, dst, to, sem, es in parts:
        rid, pid = topo.addr(to, core)
        trs.append(RemoteDMATransfer(dst_ids=[DstId(rid=rid, pnc=pid)], dma_engine_mask=_bits(es), remote_sem=sem,
                                     src=src, dst=dst))
        n += len(es)
    g.remote_dma_fused(trs, local_sem=T.sem.sent)
    return n


def _relay_program(g, core, T, topo, s):
    to = _names(topo, T, s)
    r = T.rank_of(s)
    n = 0
    for op in SCHED:
        ks = [k for k in op[1] if k in "ab"] if op[0] == "s" else []
        parts = []
        for i, k in enumerate(ks):
            g.wait_ge(T.sem["rel_" + k], _count(k))
            es = _engines(topo, core, to[k])
            step = len(es) // RELAY_ENG
            parts.append((T.rel["ab".index(k)], T.land[r], to[k], T.sem["arr_" + k], es[(step // 2) * i::step]))
        if parts:
            n += _fused(g, T, topo, core, parts)
    g.wait_ge(T.sem.sent, n)


def _vector_path(g, T, cols, blk):
    V, P, S = g.vector, g.tensor, g.scalar
    A = AluOpType
    nv = [0]

    def vi(ins):
        ins.then_inc(T.sem.vs, 1)
        nv[0] += 1

    def vsync():
        V.wait_ge(T.sem.vs, nv[0])

    def turn(q):
        V.wait_ge(T.sem["xq_%d" % q], 16)
        vi(V.transpose(T.xt[:, CW * q:CW * q + CW], T.xs[:, CW * q:CW * q + CW]))

    V.wait_ge(T.sem.gi, 2)
    vi(V.tensor_scalar(T.w1a[:, :], T.w1[:, :], 15, None, A.bitwise_and))
    vi(V.tensor_scalar(T.w1b[:, :], T.w1[:, 0:32], 31, None, A.bitwise_and))
    vi(V.tensor_scalar(T.w2a[:, :], T.w2[:, :], 4, None, A.arith_shift_right))
    vi(V.tensor_scalar(T.pq[:, :], T.w2[:, 0:1], 96, None, A.bitwise_and))
    vi(V.memset(T.xt[:, FREE:FREE + 36], 0.0))
    vsync()
    vi(V.tensor_scalar(T.rep[:, :], T.w1a[:, :], 0, None, A.is_equal))
    vi(V.tensor_scalar(T.sel[:, :], T.w1b[:, :], 0, None, A.is_equal))
    vi(V.tensor_scalar(T.dm8[:, :], T.w2a[:, :], 0, None, A.is_equal))
    vi(V.tensor_copy(T.ap32[:, :], T.pq[:, :]))
    V.wait_ge(T.sem.lq, 16)
    vi(V.tensor_copy(T.rf[:, :], T.idx[:, :]))
    vsync()
    for i, j in enumerate(cols):
        V.tensor_scalar(T.vm[:, 8 * i:8 * i + 8], T.dm8[:, :], T.rf[:, j:j + 1], None, A.mult).then_inc(T.sem.vmd, 1)
    P.wait_ge(T.sem.vmd, ND)
    P.matmul(T.pso[:, 0:8 * ND], T.rep[:, :], T.vm[:, :], True, True).then_inc(T.sem.ts, 1)
    for q in range(EARLY):
        turn(q)
    V.wait_ge(T.sem.ts, 1)
    vi(V.tensor_copy(T.rr[:, :], T.pso[:, 0:8 * ND]))
    vsync()
    vi(V.tensor_scalar(T.ta[:, :], T.rr[:, :], (ROWS - 1) - (RPC - 1), 1, A.bitwise_and, A.logical_shift_right))
    vi(V.tensor_scalar(T.tb[:, :], T.rr[:, :], (1 << KB) - 1, None, A.bitwise_and))
    vi(V.tensor_scalar(T.tc[:, :], T.rr[:, :], KB, 31, A.logical_shift_right, A.bitwise_and))
    vi(V.tensor_scalar(T.tq[:, :], T.rr[:, :], KB, 96, A.logical_shift_right, A.bitwise_and))
    vsync()
    vi(V.tensor_scalar(T.tq[:, :], T.tq[:, :], T.ap32[:, 0:1], 2 * FREE, A.not_equal, A.mult))
    vi(V.tensor_scalar(T.tb[:, :], T.tb[:, :], W, None, A.mult))
    vi(V.tensor_tensor(T.ta[:, :], T.ta[:, :], T.tc[:, :], A.add))
    vsync()
    vi(V.tensor_tensor(T.tb[:, :], T.tb[:, :], T.tq[:, :], A.add))
    vsync()
    vi(V.tensor_tensor(T.ta[:, :], T.ta[:, :], T.tb[:, :], A.add))
    vsync()
    vi(V.tensor_scalar(T.off[:, :], T.ta[:, :], FREE, None, A.min))
    for q in range(EARLY, NCH):
        turn(q)
    vsync()
    S.wait_ge(T.sem.vs, nv[0])

    def gather(s, h):
        out = T.gv[:, 512 * s + 256 * h:512 * s + 256 * h + 256]
        src = T.xt[:, 32 * h:32 * h + FREE + 4].indirect(T.off[:, 16 * s:16 * s + 16])
        ins = V.tensor_copy(out, src) if h == 0 else S.activation(out, src, ActivationFunctionType.Copy)
        ins.then_inc(T.sem["gv_%d" % s], 1)

    def leave(on_vector, k):
        (V if on_vector else S).wait_ge(T.sem["pe_" + k], 2)
        ins = (V.tensor_copy(blk(k), T["ps_" + k][:, 0:W]) if on_vector
               else S.activation(blk(k), T["ps_" + k][:, 0:W], ActivationFunctionType.Copy))
        ins.then_inc(T.sem["ev_" + k], 1)

    for s, pair in enumerate(VPAIRS):
        gather(s, 0)
        P.wait_ge(T.sem["gv_%d" % s], 2)
        for i, k in enumerate(pair):
            for h in range(2):
                at = 512 * s + 256 * h + 128 * i
                P.matmul(T["ps_" + k][:, 32 * h:32 * h + 32], T.gv[:, at:at + 128], T.sel[:, :],
                         True, True).then_inc(T.sem["pe_" + k], 1)
    last = len(VPAIRS) - 1
    gather(0, 1)
    for s in range(last):
        gather(s + 1, 1)
        for k in VPAIRS[s]:
            leave(False, k)
    for k in VPAIRS[last]:
        leave(True, k)


def rank_program(g, core, T, topo):
    rank = T.rank_of(core)
    if rank is None:
        for s in T.cores:
            if _relay_of(topo, T, s) == core:
                _relay_program(g, core, T, topo, s)
        return

    to = _names(topo, T, core)
    relay = _relay_of(topo, T, core)
    R = T.rank_of

    def blk(k):
        j = R(to[k])
        return T.gat[:, W * j:W * j + W]

    cols = [R(to[k]) for k in VLISTS]
    g.sync.dma_start(out=T.idx[:, :], in_=T.l[:, :]).then_inc(T.sem.lq, 16)
    for q in range(NCH):
        (g.scalar if q % 2 == 0 else g.sync).dma_start(out=T.xs[:, CW * q:CW * q + CW],
                                                       in_=T.x[RPC * q:RPC * q + RPC, :]).then_inc(T.sem["xq_%d" % q], 16)
    g.iota(T.w1[:, :], [[1, 128]], 128, -1).then_inc(T.sem.gi, 1)
    g.iota(T.w2[:, :], [[-16, 8]], 0, 1).then_inc(T.sem.gi, 1)
    _vector_path(g, T, cols, blk)
    g.wait_ge(T.sem.lq, 16)

    pool = _engines(topo, core, relay)
    sent = 0
    for op in SCHED:
        if op[0] == "g":
            k = op[1]
            j = R(to[k])
            g.indirect_dma_start(out=blk(k), out_offset=None, in_=T.x[:],
                                 in_offset=IndirectOffsetOnAxis(ap=T.idx[:, j:j + 1], axis=0),
                                 bounds_check=ROWS - 1, oob_is_err=True).then_inc(T.sem["gs_" + k], 16)
        else:
            parts, at = [], 0
            for k, ne in zip(op[1], op[2]):
                if k in VLISTS:
                    g.wait_ge(T.sem["ev_" + k], 1)
                else:
                    g.wait_ge(T.sem["gs_" + k], 16)
                es = pool[at:at + ne]
                at += ne
                if k in "ab":
                    parts.append((blk(k), T.rel["ab".index(k)], relay, T.sem["rel_" + k], es))
                else:
                    parts.append((blk(k), T.land[rank], to[k], T.sem["arr_" + k], es))
            sent += _fused(g, T, topo, core, parts)

    stores = [0]

    def store(q, ks):
        js = sorted(R(to[k]) for k in ks)
        for k in ks:
            q.wait_ge(T.sem["arr_" + k], RELAY_ENG if k in "ab" else _count(k))
        q.dma_start(out=T.y[CAP * js[0]:CAP * (js[-1] + 1), :], in_=T.land[js[0]:js[-1] + 1]).then_inc(T.sem.stored, 16)
        stores[0] += 1

    g.scalar.wait_ge(T.sem.ev_o, 1)
    g.scalar.dma_start(out=T.y[CAP * rank:CAP * (rank + 1), :], in_=blk("o")).then_inc(T.sem.stored, 16)
    stores[0] += 1
    store(g.sync, "ab")
    store(g.scalar, "cd")
    store(g.sync, "ef")
    store(g.scalar, "n")

    g.wait_ge(T.sem.sent, sent)
    g.wait_ge(T.sem.stored, 16 * stores[0])
